import numpy as np, ml_dtypes
CORES = [4,20,36,52,68,84,100,116,132,148,164,180,196,212,228,244]
N = 16
R, TK = 64, 16
def setup_inputs(rng):
    u = (rng.standard_normal((N, 128, R), dtype=np.float32) / 11).astype(ml_dtypes.bfloat16)
    return {"x": rng.standard_normal((N, 128, TK), dtype=np.float32).astype(ml_dtypes.bfloat16), "u": u, "ut": u.transpose(0, 2, 1).copy(), "vt": rng.standard_normal((N, R, 128), dtype=np.float32).astype(ml_dtypes.bfloat16)}
def setup_inputs_big(rng):
    d = setup_inputs(rng)
    for k in ("x", "u", "ut", "vt"): d[k] = (d[k].astype(np.float32) * 1024.0).astype(d[k].dtype)
    return d
def setup_inputs_small(rng):
    d = setup_inputs(rng)
    for k in ("x", "u", "ut", "vt"): d[k] = (d[k].astype(np.float32) * (1 / 1024.0)).astype(d[k].dtype)
    return d
def setup_inputs_apart(rng):
    d = setup_inputs(rng)
    f = (10.0 ** rng.permutation(np.linspace(-1.5, 1.5, N))).astype(np.float32).reshape(N, 1, 1)
    for k in ("x", "u", "ut", "vt"): d[k] = (d[k].astype(np.float32) * f).astype(d[k].dtype)
    return d
def tie_inputs(x):
    x = dict(x)
    x["ut"] = x["u"].transpose(0, 2, 1).copy()
    return x
def reference(x, u, ut, vt):
    X, U, VT = x.astype(np.float64), u.astype(np.float64), vt.astype(np.float64)
    y = np.stack([sum(VT[j].T @ (U[j].T @ X[r]) for j in range(N)) for r in range(N)])
    return {"y": y.astype(ml_dtypes.bfloat16 if x.dtype != np.float64 else np.float64)}

@@ -1,0 +1,79 @@
+from concourse.bass import DstId, RemoteDMATransfer
+
+NR = 16
+GS = 4
+PB = 128 // GS
+GW = 512
+
+SCRATCH = {
+    "fsend": ("dram", [128, 128], "bfloat16"),
+    "fland": ("dram", [NR, 128, 128], "bfloat16"),
+    "ft": ("sbuf", [128, (NR // GS) * GW], "bfloat16"),
+    "xs": ("sbuf", [128, 16], "bfloat16"),
+    "wb": ("sbuf", [128, 128], "bfloat16"),
+    "ys": ("sbuf", [128, 16], "bfloat16"),
+    "wp": ("psum", [128, 128], "float32"),
+    "yp": ("psum", [128, 16], "float32"),
+}
+SEMAPHORES = (["cp", "xl", "sent", "mm1", "c1", "mm2", "c2", "st"]
+              + ["arr%d" % j for j in range(NR)] + ["ld%d" % k for k in range(NR // GS)])
+
+
+def rank_program(g, core, T, topo):
+    rank = T.rank_of(core)
+    if rank is None:
+        return
+    sem = T.sem
+    cores = T.cores
+
+    g.sync.dma_start(T.fsend[0:128:2, :], T.ut[:, :]).then_inc(sem.cp, 16)
+    g.scalar.dma_start(T.fsend[1:128:2, :], T.vt[:, :]).then_inc(sem.cp, 16)
+    g.scalar.dma_start(T.xs[:, :], T.x[:, :]).then_inc(sem.xl, 16)
+
+    order = [rank ^ t for t in range(1, NR)]
+    mask = topo.mask(core, cores[order[0]])
+    ids = []
+    for d in order:
+        mask &= topo.mask(core, cores[d])
+        rid, pid = topo.addr(cores[d], core)
+        ids.append(DstId(rid=rid, pnc=pid))
+    ne = bin(mask).count("1")
+    g.wait_ge(sem.cp, 32)
+    g.remote_dma_fused(
+        [RemoteDMATransfer(dst_ids=ids, dma_engine_mask=mask, remote_sem=sem["arr%d" % rank],
+                           srcs=[T.fsend[:, :]], dsts=[T.fland[rank] for _ in order])],
+        local_sem=sem.sent)
+
+    queues = [g.sync, g.scalar]
+    for t in range(NR):
+        j = rank ^ t
+        q = queues[t % 2]
+        if t == 0:
+            q.wait_ge(sem.cp, 32)
+            src = T.fsend[:, :]
+        else:
+            q.wait_ge(sem["arr%d" % j], ne)
+            src = T.fland[j]
+        k, i = j // GS, j % GS
+        q.dma_start(T.ft[i * PB:(i + 1) * PB, k * GW:(k + 1) * GW], src).then_inc(sem["ld%d" % k], 16)
+
+    ng = NR // GS
+    for a in range(ng):
+        k = (rank // GS) ^ a
+        g.tensor.wait_ge(sem["ld%d" % k], 16 * GS)
+        for s in range(2):
+            c0 = k * GW + s * 256
+            mm = g.tensor.matmul(T.wp[:, :], T.ft[:, c0:c0 + 128], T.ft[:, c0 + 128:c0 + 256],
+                                 a == 0 and s == 0, a == ng - 1 and s == 1)
+    mm.then_inc(sem.mm1, 1)
+    g.vector.wait_ge(sem.mm1, 1)
+    g.vector.tensor_copy(T.wb[:, :], T.wp[:, :]).then_inc(sem.c1, 1)
+    g.tensor.wait_ge(sem.xl, 16)
+    g.tensor.wait_ge(sem.c1, 1)
+    g.tensor.matmul(T.yp[:, :], T.wb[:, :], T.xs[:, :], True, True).then_inc(sem.mm2, 1)
+    g.vector.wait_ge(sem.mm2, 1)
+    g.vector.tensor_copy(T.ys[:, :], T.yp[:, :]).then_inc(sem.c2, 1)
+    g.sync.wait_ge(sem.c2, 1)
+    g.sync.dma_start(T.y[:, :], T.ys[:, :]).then_inc(sem.st, 16)
+    g.sync.wait_ge(sem.st, 16)
+    g.wait_ge(sem.sent, ne)

@@ -1,79 +1,136 @@
 from concourse.bass import DstId, RemoteDMATransfer
 
 NR = 16
+HOSTS = 2
+KD = 4
+KH = 3
+ND = NR - 1 - KD - KH
 GS = 4
 PB = 128 // GS
 GW = 512
+NG = (ND + GS - 1) // GS
 
 SCRATCH = {
     "fsend": ("dram", [128, 128], "bfloat16"),
     "fland": ("dram", [NR, 128, 128], "bfloat16"),
-    "ft": ("sbuf", [128, (NR // GS) * GW], "bfloat16"),
+    "ft": ("sbuf", [128, NG * GW], "bfloat16"),
+    "uts": ("sbuf", [64, 128], "bfloat16"),
+    "vts": ("sbuf", [64, 128], "bfloat16"),
     "xs": ("sbuf", [128, 16], "bfloat16"),
+    "wown": ("sbuf", [128, 128], "bfloat16"),
+    "wl": ("sbuf", [128, NR * 128], "bfloat16"),
     "wb": ("sbuf", [128, 128], "bfloat16"),
     "ys": ("sbuf", [128, 16], "bfloat16"),
-    "wp": ("psum", [128, 128], "float32"),
-    "yp": ("psum", [128, 16], "float32"),
+    "wq": ("psum", [128, 512], "float32"),
+    "wp": ("psum", [128, 512], "float32"),
+    "yp": ("psum", [128, 512], "float32"),
 }
-SEMAPHORES = (["cp", "xl", "sent", "mm1", "c1", "mm2", "c2", "st"]
-              + ["arr%d" % j for j in range(NR)] + ["ld%d" % k for k in range(NR // GS)])
+SEMAPHORES = (["cp", "cp2", "xl", "sent", "hin", "mm0", "c0", "mm1", "c1", "mm2", "c2", "st"]
+              + ["arr%d" % j for j in range(NR)] + ["ld%d" % k for k in range(NG)])
 
 
 def rank_program(g, core, T, topo):
-    rank = T.rank_of(core)
-    if rank is None:
-        return
     sem = T.sem
     cores = T.cores
 
+    def same_chip(a, b):
+        return topo.host(a) == topo.host(b) and topo.chip(a) == topo.chip(b)
+
+    def helpers_of(c):
+        return [h for h in range(HOSTS * topo.CORES_PER_HOST)
+                if same_chip(h, c) and topo.die(h) != topo.die(c) and T.rank_of(h) is None][:KH]
+
+    def slot(j):
+        return T.wl[:, j * 128:(j + 1) * 128]
+
+    def send(dsts, src, dst, rsem, avoid):
+        mask = topo.mask(core, dsts[0])
+        ids = []
+        for d in dsts:
+            mask &= topo.mask(core, d)
+            rid, pid = topo.addr(d, core)
+            ids.append(DstId(rid=rid, pnc=pid))
+        mask &= ~avoid
+        g.remote_dma_fused(
+            [RemoteDMATransfer(dst_ids=ids, dma_engine_mask=mask, remote_sem=rsem,
+                               srcs=[src], dsts=[dst for _ in dsts])],
+            local_sem=sem.sent)
+        return bin(mask).count("1")
+
+    rank = T.rank_of(core)
+    if rank is None:
+        owners = [c for c in cores if same_chip(c, core)]
+        if not owners or core not in helpers_of(owners[0]):
+            return
+        owner = owners[0]
+        orank = T.rank_of(owner)
+        n_in = bin(topo.mask(owner, core) & ~topo.mask(owner, cores[orank ^ 1])).count("1")
+        t = ND + 1 + helpers_of(owner).index(core)
+        g.wait_ge(sem.hin, n_in)
+        n = send([cores[orank ^ t]], T.wown[:, :], slot(orank), sem["arr%d" % orank], 0)
+        g.wait_ge(sem.sent, n)
+        return
+
+    form_a = [rank ^ t for t in range(1, ND + 1)]
+    form_h = [rank ^ t for t in range(ND + 1, ND + 1 + KH)]
+    form_b = [rank ^ t for t in range(ND + 1 + KH, NR)]
+    arr = sem["arr%d" % rank]
+
     g.sync.dma_start(T.fsend[0:128:2, :], T.ut[:, :]).then_inc(sem.cp, 16)
     g.scalar.dma_start(T.fsend[1:128:2, :], T.vt[:, :]).then_inc(sem.cp, 16)
+    g.sync.dma_start(T.uts[:, :], T.ut[:, :]).then_inc(sem.cp2, 16)
+    g.scalar.dma_start(T.vts[:, :], T.vt[:, :]).then_inc(sem.cp2, 16)
     g.scalar.dma_start(T.xs[:, :], T.x[:, :]).then_inc(sem.xl, 16)
 
-    order = [rank ^ t for t in range(1, NR)]
-    mask = topo.mask(core, cores[order[0]])
-    ids = []
-    for d in order:
-        mask &= topo.mask(core, cores[d])
-        rid, pid = topo.addr(cores[d], core)
-        ids.append(DstId(rid=rid, pnc=pid))
-    ne = bin(mask).count("1")
     g.wait_ge(sem.cp, 32)
-    g.remote_dma_fused(
-        [RemoteDMATransfer(dst_ids=ids, dma_engine_mask=mask, remote_sem=sem["arr%d" % rank],
-                           srcs=[T.fsend[:, :]], dsts=[T.fland[rank] for _ in order])],
-        local_sem=sem.sent)
+    ne = send([cores[j] for j in form_a], T.fsend[:, :], T.fland[rank], arr, 0)
+    g.wait_ge(sem.c0, 1)
+    nh = send(helpers_of(core), T.wown[:, :], T.wown[:, :], sem.hin, topo.mask(core, cores[rank ^ 1]))
+    ne2 = send([cores[j] for j in form_b], T.wown[:, :], slot(rank), arr, 0)
 
     queues = [g.sync, g.scalar]
-    for t in range(NR):
-        j = rank ^ t
-        q = queues[t % 2]
-        if t == 0:
-            q.wait_ge(sem.cp, 32)
-            src = T.fsend[:, :]
-        else:
-            q.wait_ge(sem["arr%d" % j], ne)
-            src = T.fland[j]
-        k, i = j // GS, j % GS
-        q.dma_start(T.ft[i * PB:(i + 1) * PB, k * GW:(k + 1) * GW], src).then_inc(sem["ld%d" % k], 16)
+    for i, j in enumerate(form_a):
+        q = queues[i % 2]
+        q.wait_ge(sem["arr%d" % j], ne)
+        k, p = i // GS, i % GS
+        q.dma_start(T.ft[p * PB:(p + 1) * PB, k * GW:(k + 1) * GW], T.fland[j]).then_inc(sem["ld%d" % k], 16)
 
-    ng = NR // GS
-    for a in range(ng):
-        k = (rank // GS) ^ a
-        g.tensor.wait_ge(sem["ld%d" % k], 16 * GS)
+    wq, wp, yp = T.wq[:, 0:128], T.wp[:, 0:128], T.yp[:, 0:16]
+    g.tensor.wait_ge(sem.cp2, 32)
+    g.tensor.matmul(wq, T.uts[:, :], T.vts[:, :], True, True).then_inc(sem.mm0, 1)
+    g.vector.wait_ge(sem.mm0, 1)
+    g.vector.tensor_copy(T.wown[:, :], wq).then_inc(sem.c0, 1)
+
+    def group(k):
+        nb = min(GS, ND - k * GS)
+        g.tensor.wait_ge(sem["ld%d" % k], 16 * nb)
         for s in range(2):
             c0 = k * GW + s * 256
-            mm = g.tensor.matmul(T.wp[:, :], T.ft[:, c0:c0 + 128], T.ft[:, c0 + 128:c0 + 256],
-                                 a == 0 and s == 0, a == ng - 1 and s == 1)
-    mm.then_inc(sem.mm1, 1)
-    g.vector.wait_ge(sem.mm1, 1)
-    g.vector.tensor_copy(T.wb[:, :], T.wp[:, :]).then_inc(sem.c1, 1)
+            mm = g.tensor.matmul(wp, T.ft[0:nb * PB, c0:c0 + 128], T.ft[0:nb * PB, c0 + 128:c0 + 256],
+                                 k == 0 and s == 0, k == NG - 1 and s == 1)
+        return mm
+
+    def direct(j):
+        g.tensor.wait_ge(sem["arr%d" % j], ne2)
+        g.tensor.matmul(yp, slot(j), T.xs[:, :], False, False)
+
     g.tensor.wait_ge(sem.xl, 16)
+    g.tensor.wait_ge(sem.c0, 1)
+    g.tensor.matmul(yp, T.wown[:, :], T.xs[:, :], True, False)
+    for k in range(NG - 1):
+        group(k)
+    for j in form_b[:-2]:
+        direct(j)
+    group(NG - 1).then_inc(sem.mm1, 1)
+    g.vector.wait_ge(sem.mm1, 1)
+    g.vector.tensor_copy(T.wb[:, :], wp).then_inc(sem.c1, 1)
+    for j in form_b[-2:] + form_h:
+        direct(j)
     g.tensor.wait_ge(sem.c1, 1)
-    g.tensor.matmul(T.yp[:, :], T.wb[:, :], T.xs[:, :], True, True).then_inc(sem.mm2, 1)
+    g.tensor.matmul(yp, T.wb[:, :], T.xs[:, :], False, True).then_inc(sem.mm2, 1)
     g.vector.wait_ge(sem.mm2, 1)
-    g.vector.tensor_copy(T.ys[:, :], T.yp[:, :]).then_inc(sem.c2, 1)
+    g.vector.tensor_copy(T.ys[:, :], yp).then_inc(sem.c2, 1)
     g.sync.wait_ge(sem.c2, 1)
     g.sync.dma_start(T.y[:, :], T.ys[:, :]).then_inc(sem.st, 16)
     g.sync.wait_ge(sem.st, 16)
-    g.wait_ge(sem.sent, ne)
+    g.wait_ge(sem.sent, ne + nh + ne2)

@@ -3,16 +3,19 @@ from concourse.bass import DstId, RemoteDMATransfer
 NR = 16
 HOSTS = 2
 KD = 4
-KH = 3
+HC = 4
+HM = 1
+KH = HC * HM
 ND = NR - 1 - KD - KH
 GS = 4
 PB = 128 // GS
 GW = 512
 NG = (ND + GS - 1) // GS
+LOADS = [(0, 4), (4, 6), (6, 7)]
 
 SCRATCH = {
     "fsend": ("dram", [128, 128], "bfloat16"),
-    "fland": ("dram", [NR, 128, 128], "bfloat16"),
+    "fland": ("dram", [ND, 128, 128], "bfloat16"),
     "ft": ("sbuf", [128, NG * GW], "bfloat16"),
     "uts": ("sbuf", [64, 128], "bfloat16"),
     "vts": ("sbuf", [64, 128], "bfloat16"),
@@ -38,12 +41,12 @@ def rank_program(g, core, T, topo):
 
     def helpers_of(c):
         return [h for h in range(HOSTS * topo.CORES_PER_HOST)
-                if same_chip(h, c) and topo.die(h) != topo.die(c) and T.rank_of(h) is None][:KH]
+                if same_chip(h, c) and topo.die(h) != topo.die(c) and T.rank_of(h) is None][:HC]
 
     def slot(j):
         return T.wl[:, j * 128:(j + 1) * 128]
 
-    def send(dsts, src, dst, rsem, avoid):
+    def send(dsts, src, outs, rsem, avoid):
         mask = topo.mask(core, dsts[0])
         ids = []
         for d in dsts:
@@ -53,7 +56,7 @@ def rank_program(g, core, T, topo):
         mask &= ~avoid
         g.remote_dma_fused(
             [RemoteDMATransfer(dst_ids=ids, dma_engine_mask=mask, remote_sem=rsem,
-                               srcs=[src], dsts=[dst for _ in dsts])],
+                               srcs=[src], dsts=outs)],
             local_sem=sem.sent)
         return bin(mask).count("1")
 
@@ -65,9 +68,10 @@ def rank_program(g, core, T, topo):
         owner = owners[0]
         orank = T.rank_of(owner)
         n_in = bin(topo.mask(owner, core) & ~topo.mask(owner, cores[orank ^ 1])).count("1")
-        t = ND + 1 + helpers_of(owner).index(core)
+        first = ND + 1 + helpers_of(owner).index(core)
         g.wait_ge(sem.hin, n_in)
-        n = send([cores[orank ^ t]], T.wown[:, :], slot(orank), sem["arr%d" % orank], 0)
+        n = send([cores[orank ^ t] for t in range(first, ND + 1 + KH, HC)], T.wown[:, :], [slot(orank)] * HM,
+                 sem["arr%d" % orank], 0)
         g.wait_ge(sem.sent, n)
         return
 
@@ -83,17 +87,19 @@ def rank_program(g, core, T, topo):
     g.scalar.dma_start(T.xs[:, :], T.x[:, :]).then_inc(sem.xl, 16)
 
     g.wait_ge(sem.cp, 32)
-    ne = send([cores[j] for j in form_a], T.fsend[:, :], T.fland[rank], arr, 0)
+    ne = send([cores[j] for j in form_a], T.fsend[:, :], [T.fland[i] for i in range(ND)], arr, 0)
     g.wait_ge(sem.c0, 1)
-    nh = send(helpers_of(core), T.wown[:, :], T.wown[:, :], sem.hin, topo.mask(core, cores[rank ^ 1]))
-    ne2 = send([cores[j] for j in form_b], T.wown[:, :], slot(rank), arr, 0)
+    nh = send(helpers_of(core), T.wown[:, :], [T.wown[:, :]] * HC, sem.hin, topo.mask(core, cores[rank ^ 1]))
+    ne2 = send([cores[j] for j in form_b], T.wown[:, :], [slot(rank)] * KD, arr, 0)
 
     queues = [g.sync, g.scalar]
-    for i, j in enumerate(form_a):
-        q = queues[i % 2]
-        q.wait_ge(sem["arr%d" % j], ne)
-        k, p = i // GS, i % GS
-        q.dma_start(T.ft[p * PB:(p + 1) * PB, k * GW:(k + 1) * GW], T.fland[j]).then_inc(sem["ld%d" % k], 16)
+    for n, (i0, i1) in enumerate(LOADS):
+        q = queues[n % 2]
+        for j in form_a[i0:i1]:
+            q.wait_ge(sem["arr%d" % j], ne)
+        k, p = i0 // GS, i0 % GS
+        q.dma_start(T.ft[p * PB:(p + i1 - i0) * PB, k * GW:(k + 1) * GW],
+                    T.fland[i0:i1]).then_inc(sem["ld%d" % k], 16)
 
     wq, wp, yp = T.wq[:, 0:128], T.wp[:, 0:128], T.yp[:, 0:16]
     g.tensor.wait_ge(sem.cp2, 32)
@@ -103,7 +109,7 @@ def rank_program(g, core, T, topo):
 
     def group(k):
         nb = min(GS, ND - k * GS)
-        g.tensor.wait_ge(sem["ld%d" % k], 16 * nb)
+        g.tensor.wait_ge(sem["ld%d" % k], 16 * len([1 for i0, _ in LOADS if i0 // GS == k]))
         for s in range(2):
             c0 = k * GW + s * 256
             mm = g.tensor.matmul(wp, T.ft[0:nb * PB, c0:c0 + 128], T.ft[0:nb * PB, c0 + 128:c0 + 256],

from concourse.bass import DstId, RemoteDMATransfer

NR = 16
HOSTS = 2
KD = 4
HC = 4
HM = 1
KH = HC * HM
ND = NR - 1 - KD - KH
GS = 4
PB = 128 // GS
GW = 512
NG = (ND + GS - 1) // GS
LOADS = [(0, 4), (4, 6), (6, 7)]

SCRATCH = {
    "fsend": ("dram", [128, 128], "bfloat16"),
    "fland": ("dram", [ND, 128, 128], "bfloat16"),
    "ft": ("sbuf", [128, NG * GW], "bfloat16"),
    "uts": ("sbuf", [64, 128], "bfloat16"),
    "vts": ("sbuf", [64, 128], "bfloat16"),
    "xs": ("sbuf", [128, 16], "bfloat16"),
    "wown": ("sbuf", [128, 128], "bfloat16"),
    "wl": ("sbuf", [128, NR * 128], "bfloat16"),
    "wb": ("sbuf", [128, 128], "bfloat16"),
    "ys": ("sbuf", [128, 16], "bfloat16"),
    "wq": ("psum", [128, 512], "float32"),
    "wp": ("psum", [128, 512], "float32"),
    "yp": ("psum", [128, 512], "float32"),
}
SEMAPHORES = (["cp", "cp2", "xl", "sent", "hin", "mm0", "c0", "mm1", "c1", "mm2", "c2", "st"]
              + ["arr%d" % j for j in range(NR)] + ["ld%d" % k for k in range(NG)])


def rank_program(g, core, T, topo):
    sem = T.sem
    cores = T.cores

    def same_chip(a, b):
        return topo.host(a) == topo.host(b) and topo.chip(a) == topo.chip(b)

    def helpers_of(c):
        return [h for h in range(HOSTS * topo.CORES_PER_HOST)
                if same_chip(h, c) and topo.die(h) != topo.die(c) and T.rank_of(h) is None][:HC]

    def slot(j):
        return T.wl[:, j * 128:(j + 1) * 128]

    def send(dsts, src, outs, rsem, avoid):
        mask = topo.mask(core, dsts[0])
        ids = []
        for d in dsts:
            mask &= topo.mask(core, d)
            rid, pid = topo.addr(d, core)
            ids.append(DstId(rid=rid, pnc=pid))
        mask &= ~avoid
        g.remote_dma_fused(
            [RemoteDMATransfer(dst_ids=ids, dma_engine_mask=mask, remote_sem=rsem,
                               srcs=[src], dsts=outs)],
            local_sem=sem.sent)
        return bin(mask).count("1")

    rank = T.rank_of(core)
    if rank is None:
        owners = [c for c in cores if same_chip(c, core)]
        if not owners or core not in helpers_of(owners[0]):
            return
        owner = owners[0]
        orank = T.rank_of(owner)
        n_in = bin(topo.mask(owner, core) & ~topo.mask(owner, cores[orank ^ 1])).count("1")
        first = ND + 1 + helpers_of(owner).index(core)
        g.wait_ge(sem.hin, n_in)
        n = send([cores[orank ^ t] for t in range(first, ND + 1 + KH, HC)], T.wown[:, :], [slot(orank)] * HM,
                 sem["arr%d" % orank], 0)
        g.wait_ge(sem.sent, n)
        return

    form_a = [rank ^ t for t in range(1, ND + 1)]
    form_h = [rank ^ t for t in range(ND + 1, ND + 1 + KH)]
    form_b = [rank ^ t for t in range(ND + 1 + KH, NR)]
    arr = sem["arr%d" % rank]

    g.sync.dma_start(T.fsend[0:128:2, :], T.ut[:, :]).then_inc(sem.cp, 16)
    g.scalar.dma_start(T.fsend[1:128:2, :], T.vt[:, :]).then_inc(sem.cp, 16)
    g.sync.dma_start(T.uts[:, :], T.ut[:, :]).then_inc(sem.cp2, 16)
    g.scalar.dma_start(T.vts[:, :], T.vt[:, :]).then_inc(sem.cp2, 16)
    g.scalar.dma_start(T.xs[:, :], T.x[:, :]).then_inc(sem.xl, 16)

    g.wait_ge(sem.cp, 32)
    ne = send([cores[j] for j in form_a], T.fsend[:, :], [T.fland[i] for i in range(ND)], arr, 0)
    g.wait_ge(sem.c0, 1)
    nh = send(helpers_of(core), T.wown[:, :], [T.wown[:, :]] * HC, sem.hin, topo.mask(core, cores[rank ^ 1]))
    ne2 = send([cores[j] for j in form_b], T.wown[:, :], [slot(rank)] * KD, arr, 0)

    queues = [g.sync, g.scalar]
    for n, (i0, i1) in enumerate(LOADS):
        q = queues[n % 2]
        for j in form_a[i0:i1]:
            q.wait_ge(sem["arr%d" % j], ne)
        k, p = i0 // GS, i0 % GS
        q.dma_start(T.ft[p * PB:(p + i1 - i0) * PB, k * GW:(k + 1) * GW],
                    T.fland[i0:i1]).then_inc(sem["ld%d" % k], 16)

    wq, wp, yp = T.wq[:, 0:128], T.wp[:, 0:128], T.yp[:, 0:16]
    g.tensor.wait_ge(sem.cp2, 32)
    g.tensor.matmul(wq, T.uts[:, :], T.vts[:, :], True, True).then_inc(sem.mm0, 1)
    g.vector.wait_ge(sem.mm0, 1)
    g.vector.tensor_copy(T.wown[:, :], wq).then_inc(sem.c0, 1)

    def group(k):
        nb = min(GS, ND - k * GS)
        g.tensor.wait_ge(sem["ld%d" % k], 16 * len([1 for i0, _ in LOADS if i0 // GS == k]))
        for s in range(2):
            c0 = k * GW + s * 256
            mm = g.tensor.matmul(wp, T.ft[0:nb * PB, c0:c0 + 128], T.ft[0:nb * PB, c0 + 128:c0 + 256],
                                 k == 0 and s == 0, k == NG - 1 and s == 1)
        return mm

    def direct(j):
        g.tensor.wait_ge(sem["arr%d" % j], ne2)
        g.tensor.matmul(yp, slot(j), T.xs[:, :], False, False)

    g.tensor.wait_ge(sem.xl, 16)
    g.tensor.wait_ge(sem.c0, 1)
    g.tensor.matmul(yp, T.wown[:, :], T.xs[:, :], True, False)
    for k in range(NG - 1):
        group(k)
    for j in form_b[:-2]:
        direct(j)
    group(NG - 1).then_inc(sem.mm1, 1)
    g.vector.wait_ge(sem.mm1, 1)
    g.vector.tensor_copy(T.wb[:, :], wp).then_inc(sem.c1, 1)
    for j in form_b[-2:] + form_h:
        direct(j)
    g.tensor.wait_ge(sem.c1, 1)
    g.tensor.matmul(yp, T.wb[:, :], T.xs[:, :], False, True).then_inc(sem.mm2, 1)
    g.vector.wait_ge(sem.mm2, 1)
    g.vector.tensor_copy(T.ys[:, :], yp).then_inc(sem.c2, 1)
    g.sync.wait_ge(sem.c2, 1)
    g.sync.dma_start(T.y[:, :], T.ys[:, :]).then_inc(sem.st, 16)
    g.sync.wait_ge(sem.st, 16)
    g.wait_ge(sem.sent, ne + nh + ne2)
